import numpy as np
import ml_dtypes


def mxq(x, axis, fmt="e4m3"):
    dtype, down = {"e4m3": (ml_dtypes.float8_e4m3fn, 7), "e5m2": (ml_dtypes.float8_e5m2, 14)}[fmt]
    v = np.moveaxis(np.asarray(x, np.float32).astype(ml_dtypes.bfloat16).astype(np.float64), axis, -1)
    blocks = v.reshape(v.shape[:-1] + (-1, 32))
    amax = np.abs(blocks).max(-1, keepdims=True)
    byte = np.maximum(np.where(amax > 0, np.frexp(amax)[1] - 1 + 127, 0) - down, 1)
    scale = np.exp2(byte - 127.0)
    codes = (blocks / scale).astype(np.float32).astype(dtype).astype(np.float64)
    return np.moveaxis((codes * scale).reshape(v.shape), -1, axis)


WIDE = False


def mx_kscale(k):
    if not WIDE:
        return np.ones(k)
    levels = np.array([10, -10, 5, -5, 0])
    if k % 512:
        return np.exp2(np.random.permutation(np.resize(levels, k // 32))).repeat(32)
    a = np.empty((k // 512, 16))
    for p in range(k // 512):
        a[p, :8] = np.random.permutation(np.resize(levels, 8))
        for g in range(8):
            far = levels[np.abs(levels - a[p, g]) >= 10]
            a[p, g + 8] = far[np.random.randint(len(far))]
    return np.exp2(a.ravel()).repeat(32)


def f64(x):
    return np.asarray(x).astype(np.float64)


def striped(idx):
    return np.tile(idx.reshape(-1, 16).T, (8, 1)).astype(np.uint16)


def unstriped(offs):
    return offs[:16].T.reshape(-1).astype(np.int64)


def relu(v):
    return np.maximum(v, 0.0)


K, T, D, S, V, N = 1024, 2048, 4, 1024, 512, 128


def setup_inputs():
    n = np.random.standard_normal
    s = mx_kscale(K)[:, None]
    return {
        "xT": (n((K, T)) * s).astype(np.float32),
        "w": (n((K, N)) / np.sqrt(K) / s).astype(np.float32),
        "b": (0.3 * n((N, 1))).astype(np.float32),
        "gate": np.tile(np.random.uniform(0.2, 1.0, (D, 1, V)) / np.sqrt(D), (1, N, 1)).astype(np.float32),
        "offs": striped(np.random.permutation(T)[:S]),
        "pos1": striped(np.random.permutation(S)[:V]),
        "pos2": striped(np.random.permutation(S)[:V]),
        "pos3": striped(np.random.permutation(S)[:V]),
        "pos4": striped(np.random.permutation(S)[:V]),
    }


def reference(xT, w, b, gate, offs, pos1, pos2, pos3, pos4):
    idx = unstriped(offs)
    xq = mxq(f64(xT)[:, idx], 0, "e4m3")
    y = mxq(f64(w), 0, "e4m3").T @ xq
    y = relu(y + f64(b))
    return sum(f64(gate[d]) * y[:, unstriped(p)] for d, p in enumerate((pos1, pos2, pos3, pos4)))

@@ -1,0 +1,198 @@
+from contextlib import ExitStack
+
+import concourse.mybir as mybir
+
+K, T, D, S, V, N = 1024, 2048, 4, 1024, 512, 128
+FLOPS = 2 * K * S * N + 2 * D * V * N
+
+F32 = mybir.dt.float32
+BF16 = mybir.dt.bfloat16
+U32 = mybir.dt.uint32
+U16 = mybir.dt.uint16
+U8 = mybir.dt.uint8
+FP8X4 = mybir.dt.float8_e4m3fn_x4
+COPY = mybir.ActivationFunctionType.Copy
+RELU = mybir.ActivationFunctionType.Relu
+ADD = mybir.AluOpType.add
+MAX = mybir.AluOpType.max
+MULT = mybir.AluOpType.mult
+
+P = 128
+PASSES = 2
+
+LOADS = {
+    (0, 0): [(256, 0), (256, 0), (512, 128), (1024, 256)],
+    (0, 1): [(1024, 256), (1024, 256)],
+    (1, 0): [(1024, 256), (1024, 256)],
+    (1, 1): [(1024, 256), (512, 192), (256, 112), (256, 144)],
+}
+
+
+def tile_picked_sub_lin_relu_sub_e_kernel(tc, xT, w, b, gate, offs, pos1, pos2, pos3, pos4, out):
+    nc = tc.nc
+    with ExitStack() as ctx:
+        keep = ctx.enter_context(tc.tile_pool(name="keep", bufs=1))
+        psum = ctx.enter_context(tc.psum_pool(name="psum", bufs=1))
+
+        warm = keep.tile([P, 1], F32, name="warm")
+        warm_out = keep.tile([P, 1], F32, name="warm_out")
+        nc.vector.memset(warm[:], 0.0)
+        nc.scalar.activation(warm_out[:], warm[:], RELU)
+
+        offs_sb = keep.tile([P, S // 16], U16, name="offs_sb")
+        pos_sb = [keep.tile([P, V // 16], U16, name=f"pos_sb{d}") for d in range(D)]
+        b_sb = keep.tile([P, 1], F32, name="b_sb")
+        w_raw = keep.tile([P, PASSES, 4, N], F32, name="w_raw")
+        gate_sb = keep.tile([P, D, V], F32, name="gate_sb")
+
+        raw = {}
+        for (a, u), loads in LOADS.items():
+            rows = xT[512 * a : 512 * (a + 1), :].rearrange("(p j) t -> p j t", j=4)
+            t0 = 0
+            for i, (n, nv) in enumerate(loads):
+                tile = keep.tile([P, 2, n], F32, name=f"raw_{a}{u}_{i}")
+                nc.sync.dma_start(tile[:], rows[:, 2 * u : 2 * u + 2, t0 : t0 + n])
+                raw[a, u, i] = tile
+                t0 += n
+            if (a, u) == (0, 0):
+                nc.sync.dma_start(offs_sb[:], offs)
+                nc.sync.dma_start(b_sb[:], b)
+            if (a, u) == (1, 0):
+                for tile, pos in zip(pos_sb, (pos1, pos2, pos3, pos4)):
+                    nc.sync.dma_start(tile[:], pos)
+        nc.sync.dma_start(w_raw[:], w.rearrange("(a p j) m -> p a j m", a=PASSES, j=4))
+        nc.sync.dma_start(gate_sb[:], gate.rearrange("d m v -> m d v"))
+
+        pair = {}
+        for a in range(PASSES):
+            for u in range(2):
+                pair[a, u] = keep.tile([P, T, 2], BF16, name=f"pair_{a}{u}", align_bytes=64)
+        G0, G1 = 512, 256
+        picked = {}
+        for a, g in ((0, G0), (1, G1)):
+            for s in range(S // g):
+                picked[a, s] = keep.tile([P, g, 4], BF16, name=f"picked_{a}_{s}", align_bytes=64)
+        x_codes = [keep.tile([P, S], U32, name=f"x_codes{a}", align_bytes=64) for a in range(PASSES)]
+        x_scales = [keep.tile([P, S], U8, name=f"x_scales{a}", align_bytes=64) for a in range(PASSES)]
+        w_bf = keep.tile([P, PASSES, N, 4], BF16, name="w_bf", align_bytes=64)
+        w_codes = keep.tile([P, PASSES * N], U32, name="w_codes", align_bytes=64)
+        w_scales = keep.tile([P, PASSES * N], U8, name="w_scales", align_bytes=64)
+
+        def cast(a, u):
+            t0 = 0
+            for i, (n, nv) in enumerate(LOADS[a, u]):
+                src = raw[a, u, i]
+                ns = n - nv
+                nc.scalar.activation(
+                    pair[a, u][:, t0 : t0 + ns, :], src[:, :, :ns].rearrange("p e t -> p t e"), COPY
+                )
+                if nv:
+                    nc.vector.tensor_copy(
+                        pair[a, u][:, t0 + ns : t0 + n, :], src[:, :, ns:].rearrange("p e t -> p t e")
+                    )
+                t0 += n
+
+        def gather(a, u, s):
+            g = G0 if a == 0 else G1
+            words = pair[a, u][:].rearrange("p t e -> p (t e)").bitcast(U32)
+            dst = picked[a, s][:].rearrange("p s j -> p (s j)").bitcast(U32).rearrange("p (s u) -> p s u", u=2)
+            nc.vector.tensor_copy(dst[:, :, u], words.indirect(offs_sb[:, g // 16 * s : g // 16 * (s + 1)]))
+
+        def quantize(a, tile, e0, e1, c0):
+            n = e1 - e0
+            nc.vector.quantize_mx(
+                out=x_codes[a][:, c0 : c0 + n].bitcast(FP8X4),
+                scales=x_scales[a][:, c0 : c0 + n],
+                in_=tile[:, e0:e1, :].rearrange("p s j -> p (s j)"),
+            )
+
+        cast(0, 0)
+        gather(0, 0, 0)
+        gather(0, 0, 1)
+        cast(0, 1)
+        gather(0, 1, 0)
+        gather(0, 1, 1)
+        cast(1, 0)
+        quantize(0, picked[0, 0], 0, 512, 0)
+        quantize(0, picked[0, 1], 0, 512, 512)
+        for s in range(4):
+            gather(1, 0, s)
+        cast(1, 1)
+        for a in range(PASSES):
+            nc.scalar.activation(w_bf[:, a], w_raw[:, a].rearrange("p j m -> p m j"), COPY)
+
+        def quantize_w():
+            nc.vector.quantize_mx(
+                out=w_codes[:].bitcast(FP8X4), scales=w_scales[:], in_=w_bf[:].rearrange("p a m j -> p (a m j)")
+            )
+
+        gather(1, 1, 0)
+        gather(1, 1, 1)
+        quantize(1, picked[1, 0], 0, 256, 0)
+        gather(1, 1, 2)
+        quantize(1, picked[1, 1], 0, 256, 256)
+        quantize_w()
+        gather(1, 1, 3)
+        quantize(1, picked[1, 2], 0, 256, 512)
+        quantize(1, picked[1, 3], 0, 128, 768)
+        quantize(1, picked[1, 3], 128, 256, 896)
+
+        y = keep.tile([P, S], F32, name="y")
+        slices = [(0, 256), (256, 256), (512, 256), (768, 128), (896, 128)]
+        banks = [psum.tile([P, n], F32, name=f"bank{i}") for i, (c0, n) in enumerate(slices)]
+        for a in range(PASSES):
+            for bank, (c0, n) in zip(banks, slices):
+                nc.tensor.matmul_mx(
+                    out=bank[:],
+                    lhsT=w_codes[:, N * a : N * (a + 1)].bitcast(FP8X4),
+                    lhsT_scale=w_scales[:, N * a : N * (a + 1)],
+                    rhs=x_codes[a][:, c0 : c0 + n].bitcast(FP8X4),
+                    rhs_scale=x_scales[a][:, c0 : c0 + n],
+                    start=(a == 0),
+                    stop=(a == PASSES - 1),
+                )
+        for i, (bank, (c0, n)) in enumerate(zip(banks, slices)):
+            if i < 4:
+                nc.scalar.activation(y[:, c0 : c0 + n], bank[:], RELU, bias=b_sb[:])
+            else:
+                nc.vector.tensor_scalar(y[:, c0 : c0 + n], bank[:], b_sb[:], 0.0, ADD, MAX)
+
+        H = V // 2
+        prod = {}
+        for h in range(2):
+            for d in range(D):
+                prod[d, h] = keep.tile([P, H], F32, name=f"prod_{d}_{h}")
+
+        def fetch(d, h):
+            nc.vector.tensor_tensor(
+                prod[d, h][:],
+                y[:].indirect(pos_sb[d][:, H // 16 * h : H // 16 * (h + 1)]),
+                gate_sb[:, d, H * h : H * (h + 1)],
+                MULT,
+            )
+
+        sums = {}
+        for h in range(2):
+            for i in range(3):
+                sums[i, h] = keep.tile([P, H], F32, name=f"sum_{i}_{h}")
+
+        def add(i, h):
+            lhs = prod[0, h] if i == 0 else sums[i - 1, h]
+            nc.vector.tensor_tensor(sums[i, h][:], lhs[:], prod[i + 1, h][:], ADD)
+
+        fetch(0, 0)
+        fetch(1, 0)
+        fetch(2, 0)
+        add(0, 0)
+        fetch(3, 0)
+        add(1, 0)
+        fetch(0, 1)
+        add(2, 0)
+        nc.sync.dma_start(out[:, :H], sums[2, 0][:])
+        fetch(1, 1)
+        fetch(2, 1)
+        add(0, 1)
+        fetch(3, 1)
+        add(1, 1)
+        add(2, 1)
+        nc.sync.dma_start(out[:, H:], sums[2, 1][:])

@@ -21,10 +21,10 @@ P = 128
 PASSES = 2
 
 LOADS = {
-    (0, 0): [(256, 0), (256, 0), (512, 128), (1024, 256)],
-    (0, 1): [(1024, 256), (1024, 256)],
-    (1, 0): [(1024, 256), (1024, 256)],
-    (1, 1): [(1024, 256), (512, 192), (256, 112), (256, 144)],
+    (0, 0): [(512, 320), (512, 320), (512, 320), (512, 320)],
+    (0, 1): [(512, 0), (512, 0), (512, 64), (512, 64)],
+    (1, 0): [(1024, 0), (1024, 128)],
+    (1, 1): [(512, 0), (512, 64), (512, 128), (256, 96), (256, 144)],
 }
 
 
@@ -56,12 +56,15 @@ def tile_picked_sub_lin_relu_sub_e_kernel(tc, xT, w, b, gate, offs, pos1, pos2, 
                 t0 += n
             if (a, u) == (0, 0):
                 nc.sync.dma_start(offs_sb[:], offs)
-                nc.sync.dma_start(b_sb[:], b)
-            if (a, u) == (1, 0):
-                for tile, pos in zip(pos_sb, (pos1, pos2, pos3, pos4)):
-                    nc.sync.dma_start(tile[:], pos)
-        nc.sync.dma_start(w_raw[:], w.rearrange("(a p j) m -> p a j m", a=PASSES, j=4))
-        nc.sync.dma_start(gate_sb[:], gate.rearrange("d m v -> m d v"))
+                nc.sync.dma_start(w_raw[:], w.rearrange("(a p j) m -> p a j m", a=PASSES, j=4))
+        nc.sync.dma_start(b_sb[:], b)
+        for tile, pos in zip(pos_sb, (pos1, pos2, pos3, pos4)):
+            nc.sync.dma_start(tile[:], pos)
+        for h in range(2):
+            nc.sync.dma_start(
+                gate_sb[:, :, V // 2 * h : V // 2 * (h + 1)],
+                gate.rearrange("d m v -> m d v")[:, :, V // 2 * h : V // 2 * (h + 1)],
+            )
 
         pair = {}
         for a in range(PASSES):
@@ -110,6 +113,11 @@ def tile_picked_sub_lin_relu_sub_e_kernel(tc, xT, w, b, gate, offs, pos1, pos2, 
         gather(0, 0, 0)
         gather(0, 0, 1)
         cast(0, 1)
+        for a in range(PASSES):
+            nc.scalar.activation(w_bf[:, a], w_raw[:, a].rearrange("p j m -> p m j"), COPY)
+        nc.vector.quantize_mx(
+            out=w_codes[:].bitcast(FP8X4), scales=w_scales[:], in_=w_bf[:].rearrange("p a m j -> p (a m j)")
+        )
         gather(0, 1, 0)
         gather(0, 1, 1)
         cast(1, 0)
@@ -118,20 +126,11 @@ def tile_picked_sub_lin_relu_sub_e_kernel(tc, xT, w, b, gate, offs, pos1, pos2, 
         for s in range(4):
             gather(1, 0, s)
         cast(1, 1)
-        for a in range(PASSES):
-            nc.scalar.activation(w_bf[:, a], w_raw[:, a].rearrange("p j m -> p m j"), COPY)
-
-        def quantize_w():
-            nc.vector.quantize_mx(
-                out=w_codes[:].bitcast(FP8X4), scales=w_scales[:], in_=w_bf[:].rearrange("p a m j -> p (a m j)")
-            )
-
         gather(1, 1, 0)
         gather(1, 1, 1)
         quantize(1, picked[1, 0], 0, 256, 0)
         gather(1, 1, 2)
         quantize(1, picked[1, 1], 0, 256, 256)
-        quantize_w()
         gather(1, 1, 3)
         quantize(1, picked[1, 2], 0, 256, 512)
         quantize(1, picked[1, 3], 0, 128, 768)
@@ -158,41 +157,29 @@ def tile_picked_sub_lin_relu_sub_e_kernel(tc, xT, w, b, gate, offs, pos1, pos2, 
                 nc.vector.tensor_scalar(y[:, c0 : c0 + n], bank[:], b_sb[:], 0.0, ADD, MAX)
 
         H = V // 2
-        prod = {}
-        for h in range(2):
-            for d in range(D):
-                prod[d, h] = keep.tile([P, H], F32, name=f"prod_{d}_{h}")
+        prod = [keep.tile([P, V], F32, name=f"prod_{d}") for d in range(D)]
+        sums = [keep.tile([P, V], F32, name=f"sum_{i}") for i in range(D - 1)]
 
-        def fetch(d, h):
+        def fetch(d, v0, v1):
             nc.vector.tensor_tensor(
-                prod[d, h][:],
-                y[:].indirect(pos_sb[d][:, H // 16 * h : H // 16 * (h + 1)]),
-                gate_sb[:, d, H * h : H * (h + 1)],
+                prod[d][:, v0:v1],
+                y[:].indirect(pos_sb[d][:, v0 // 16 : v1 // 16]),
+                gate_sb[:, d, v0:v1],
                 MULT,
             )
 
-        sums = {}
-        for h in range(2):
-            for i in range(3):
-                sums[i, h] = keep.tile([P, H], F32, name=f"sum_{i}_{h}")
+        def add(i, v0, v1):
+            lhs = prod[0] if i == 0 else sums[i - 1]
+            nc.vector.tensor_tensor(sums[i][:, v0:v1], lhs[:, v0:v1], prod[i + 1][:, v0:v1], ADD)
 
-        def add(i, h):
-            lhs = prod[0, h] if i == 0 else sums[i - 1, h]
-            nc.vector.tensor_tensor(sums[i, h][:], lhs[:], prod[i + 1, h][:], ADD)
-
-        fetch(0, 0)
-        fetch(1, 0)
-        fetch(2, 0)
-        add(0, 0)
-        fetch(3, 0)
-        add(1, 0)
-        fetch(0, 1)
-        add(2, 0)
-        nc.sync.dma_start(out[:, :H], sums[2, 0][:])
-        fetch(1, 1)
-        fetch(2, 1)
-        add(0, 1)
-        fetch(3, 1)
-        add(1, 1)
-        add(2, 1)
-        nc.sync.dma_start(out[:, H:], sums[2, 1][:])
+        fetch(0, 0, V)
+        fetch(1, 0, V)
+        fetch(2, 0, V)
+        add(0, 0, V)
+        fetch(3, 0, H)
+        add(1, 0, V)
+        fetch(3, H, V)
+        add(2, 0, H)
+        nc.sync.dma_start(out[:, :H], sums[2][:, :H])
+        add(2, H, V)
+        nc.scalar.dma_start(out[:, H:], sums[2][:, H:])

@@ -42,7 +42,7 @@ def tile_picked_sub_lin_relu_sub_e_kernel(tc, xT, w, b, gate, offs, pos1, pos2, 
         offs_sb = keep.tile([P, S // 16], U16, name="offs_sb")
         pos_sb = [keep.tile([P, V // 16], U16, name=f"pos_sb{d}") for d in range(D)]
         b_sb = keep.tile([P, 1], F32, name="b_sb")
-        w_raw = keep.tile([P, PASSES, 4, N], F32, name="w_raw")
+        w_raw = [keep.tile([P, 4, N], F32, name=f"w_raw{a}") for a in range(PASSES)]
         gate_sb = keep.tile([P, D, V], F32, name="gate_sb")
 
         raw = {}
@@ -56,7 +56,8 @@ def tile_picked_sub_lin_relu_sub_e_kernel(tc, xT, w, b, gate, offs, pos1, pos2, 
                 t0 += n
             if (a, u) == (0, 0):
                 nc.sync.dma_start(offs_sb[:], offs)
-                nc.sync.dma_start(w_raw[:], w.rearrange("(a p j) m -> p a j m", a=PASSES, j=4))
+        for a in range(PASSES):
+            nc.sync.dma_start(w_raw[a][:], w[512 * a : 512 * (a + 1), :].rearrange("(p j) m -> p j m", j=4))
         nc.sync.dma_start(b_sb[:], b)
         for tile, pos in zip(pos_sb, (pos1, pos2, pos3, pos4)):
             nc.sync.dma_start(tile[:], pos)
@@ -77,9 +78,9 @@ def tile_picked_sub_lin_relu_sub_e_kernel(tc, xT, w, b, gate, offs, pos1, pos2, 
                 picked[a, s] = keep.tile([P, g, 4], BF16, name=f"picked_{a}_{s}", align_bytes=64)
         x_codes = [keep.tile([P, S], U32, name=f"x_codes{a}", align_bytes=64) for a in range(PASSES)]
         x_scales = [keep.tile([P, S], U8, name=f"x_scales{a}", align_bytes=64) for a in range(PASSES)]
-        w_bf = keep.tile([P, PASSES, N, 4], BF16, name="w_bf", align_bytes=64)
-        w_codes = keep.tile([P, PASSES * N], U32, name="w_codes", align_bytes=64)
-        w_scales = keep.tile([P, PASSES * N], U8, name="w_scales", align_bytes=64)
+        w_bf = [keep.tile([P, N, 4], BF16, name=f"w_bf{a}", align_bytes=64) for a in range(PASSES)]
+        w_codes = [keep.tile([P, N], U32, name=f"w_codes{a}", align_bytes=64) for a in range(PASSES)]
+        w_scales = [keep.tile([P, N], U8, name=f"w_scales{a}", align_bytes=64) for a in range(PASSES)]
 
         def cast(a, u):
             t0 = 0
@@ -113,11 +114,6 @@ def tile_picked_sub_lin_relu_sub_e_kernel(tc, xT, w, b, gate, offs, pos1, pos2, 
         gather(0, 0, 0)
         gather(0, 0, 1)
         cast(0, 1)
-        for a in range(PASSES):
-            nc.scalar.activation(w_bf[:, a], w_raw[:, a].rearrange("p j m -> p m j"), COPY)
-        nc.vector.quantize_mx(
-            out=w_codes[:].bitcast(FP8X4), scales=w_scales[:], in_=w_bf[:].rearrange("p a m j -> p (a m j)")
-        )
         gather(0, 1, 0)
         gather(0, 1, 1)
         cast(1, 0)
@@ -126,12 +122,30 @@ def tile_picked_sub_lin_relu_sub_e_kernel(tc, xT, w, b, gate, offs, pos1, pos2, 
         for s in range(4):
             gather(1, 0, s)
         cast(1, 1)
-        gather(1, 1, 0)
-        gather(1, 1, 1)
-        quantize(1, picked[1, 0], 0, 256, 0)
+        for a in range(PASSES):
+            nc.scalar.activation(w_bf[a][:], w_raw[a][:].rearrange("p j m -> p m j"), COPY)
+
+        def quantize_w(a):
+            nc.vector.quantize_mx(
+                out=w_codes[a][:].bitcast(FP8X4), scales=w_scales[a][:], in_=w_bf[a][:].rearrange("p m j -> p (m j)")
+            )
+
+        def gather_and_spread(s):
+            near = keep.tile([P, G1, 2], BF16, name=f"near_{s}", align_bytes=64)
+            nc.vector.tensor_copy(
+                near[:].rearrange("p s e -> p (s e)").bitcast(U32),
+                pair[1, 1][:].rearrange("p t e -> p (t e)").bitcast(U32).indirect(offs_sb[:, G1 // 16 * s : G1 // 16 * (s + 1)]),
+            )
+            nc.scalar.copy(picked[1, s][:, :, 2:4], near[:])
+
+        gather_and_spread(0)
+        gather_and_spread(1)
         gather(1, 1, 2)
-        quantize(1, picked[1, 1], 0, 256, 256)
+        quantize_w(0)
         gather(1, 1, 3)
+        quantize(1, picked[1, 0], 0, 256, 0)
+        quantize_w(1)
+        quantize(1, picked[1, 1], 0, 256, 256)
         quantize(1, picked[1, 2], 0, 256, 512)
         quantize(1, picked[1, 3], 0, 128, 768)
         quantize(1, picked[1, 3], 128, 256, 896)
@@ -143,8 +157,8 @@ def tile_picked_sub_lin_relu_sub_e_kernel(tc, xT, w, b, gate, offs, pos1, pos2, 
             for bank, (c0, n) in zip(banks, slices):
                 nc.tensor.matmul_mx(
                     out=bank[:],
-                    lhsT=w_codes[:, N * a : N * (a + 1)].bitcast(FP8X4),
-                    lhsT_scale=w_scales[:, N * a : N * (a + 1)],
+                    lhsT=w_codes[a][:].bitcast(FP8X4),
+                    lhsT_scale=w_scales[a][:],
                     rhs=x_codes[a][:, c0 : c0 + n].bitcast(FP8X4),
                     rhs_scale=x_scales[a][:, c0 : c0 + n],
                     start=(a == 0),

@@ -22,9 +22,9 @@ PASSES = 2
 
 LOADS = {
     (0, 0): [(512, 320), (512, 320), (512, 320), (512, 320)],
-    (0, 1): [(512, 0), (512, 0), (512, 64), (512, 64)],
-    (1, 0): [(1024, 0), (1024, 128)],
-    (1, 1): [(512, 0), (512, 64), (512, 128), (256, 96), (256, 144)],
+    (0, 1): [(512, 128), (512, 160), (512, 160), (512, 352)],
+    (1, 0): [(512, 0), (512, 0), (512, 64), (512, 192)],
+    (1, 1): [(512, 0), (512, 0), (512, 256), (256, 0), (256, 256)],
 }
 
 
@@ -87,9 +87,10 @@ def tile_picked_sub_lin_relu_sub_e_kernel(tc, xT, w, b, gate, offs, pos1, pos2, 
             for i, (n, nv) in enumerate(LOADS[a, u]):
                 src = raw[a, u, i]
                 ns = n - nv
-                nc.scalar.activation(
-                    pair[a, u][:, t0 : t0 + ns, :], src[:, :, :ns].rearrange("p e t -> p t e"), COPY
-                )
+                if ns:
+                    nc.scalar.activation(
+                        pair[a, u][:, t0 : t0 + ns, :], src[:, :, :ns].rearrange("p e t -> p t e"), COPY
+                    )
                 if nv:
                     nc.vector.tensor_copy(
                         pair[a, u][:, t0 + ns : t0 + n, :], src[:, :, ns:].rearrange("p e t -> p t e")
@@ -140,11 +141,11 @@ def tile_picked_sub_lin_relu_sub_e_kernel(tc, xT, w, b, gate, offs, pos1, pos2, 
 
         gather_and_spread(0)
         gather_and_spread(1)
-        gather(1, 1, 2)
         quantize_w(0)
+        gather(1, 1, 2)
+        quantize_w(1)
         gather(1, 1, 3)
         quantize(1, picked[1, 0], 0, 256, 0)
-        quantize_w(1)
         quantize(1, picked[1, 1], 0, 256, 256)
         quantize(1, picked[1, 2], 0, 256, 512)
         quantize(1, picked[1, 3], 0, 128, 768)
@@ -170,7 +171,7 @@ def tile_picked_sub_lin_relu_sub_e_kernel(tc, xT, w, b, gate, offs, pos1, pos2, 
             else:
                 nc.vector.tensor_scalar(y[:, c0 : c0 + n], bank[:], b_sb[:], 0.0, ADD, MAX)
 
-        H = V // 2
+        H = 384
         prod = [keep.tile([P, V], F32, name=f"prod_{d}") for d in range(D)]
         sums = [keep.tile([P, V], F32, name=f"sum_{i}") for i in range(D - 1)]
 
@@ -190,9 +191,9 @@ def tile_picked_sub_lin_relu_sub_e_kernel(tc, xT, w, b, gate, offs, pos1, pos2, 
         fetch(1, 0, V)
         fetch(2, 0, V)
         add(0, 0, V)
-        fetch(3, 0, H)
-        add(1, 0, V)
-        fetch(3, H, V)
+        fetch(3, 0, V)
+        add(1, 0, H)
+        add(1, H, V)
         add(2, 0, H)
         nc.sync.dma_start(out[:, :H], sums[2][:, :H])
         add(2, H, V)

@@ -19,13 +19,23 @@ MULT = mybir.AluOpType.mult
 
 P = 128
 PASSES = 2
+K_PASS = K // PASSES
+LIST_ROWS = 16
 
 LOADS = {
     (0, 0): [(512, 320), (512, 320), (512, 320), (512, 320)],
-    (0, 1): [(512, 128), (512, 160), (512, 160), (512, 352)],
-    (1, 0): [(512, 0), (512, 0), (512, 64), (512, 192)],
-    (1, 1): [(512, 0), (512, 0), (512, 256), (256, 0), (256, 256)],
+    (0, 1): [(512, 128), (512, 160), (512, 128), (512, 288)],
+    (1, 0): [(512, 0), (512, 0), (512, 0), (512, 192)],
+    (1, 1): [(512, 0), (512, 0), (512, 256), (256, 0), (256, 128)],
 }
+
+SLICE0 = 512
+SLICE1 = 256
+SPREAD = 2
+
+BANKS = [(0, 256), (256, 256), (512, 256), (768, 128), (896, 128)]
+
+SPLIT = 384
 
 
 def tile_picked_sub_lin_relu_sub_e_kernel(tc, xT, w, b, gate, offs, pos1, pos2, pos3, pos4, out):
@@ -39,162 +49,148 @@ def tile_picked_sub_lin_relu_sub_e_kernel(tc, xT, w, b, gate, offs, pos1, pos2, 
         nc.vector.memset(warm[:], 0.0)
         nc.scalar.activation(warm_out[:], warm[:], RELU)
 
-        offs_sb = keep.tile([P, S // 16], U16, name="offs_sb")
-        pos_sb = [keep.tile([P, V // 16], U16, name=f"pos_sb{d}") for d in range(D)]
+        offs_sb = keep.tile([P, S // LIST_ROWS], U16, name="offs_sb")
+        pos_sb = [keep.tile([P, V // LIST_ROWS], U16, name=f"pos_sb{d}") for d in range(D)]
         b_sb = keep.tile([P, 1], F32, name="b_sb")
         w_raw = [keep.tile([P, 4, N], F32, name=f"w_raw{a}") for a in range(PASSES)]
         gate_sb = keep.tile([P, D, V], F32, name="gate_sb")
 
         raw = {}
         for (a, u), loads in LOADS.items():
-            rows = xT[512 * a : 512 * (a + 1), :].rearrange("(p j) t -> p j t", j=4)
+            rows = xT[K_PASS * a : K_PASS * (a + 1), :].rearrange("(p j) t -> p j t", j=4)
             t0 = 0
-            for i, (n, nv) in enumerate(loads):
-                tile = keep.tile([P, 2, n], F32, name=f"raw_{a}{u}_{i}")
-                nc.sync.dma_start(tile[:], rows[:, 2 * u : 2 * u + 2, t0 : t0 + n])
-                raw[a, u, i] = tile
+            for i, (n, n_vector) in enumerate(loads):
+                nodes = keep.tile([P, 2, n], F32, name=f"raw_{a}{u}_{i}")
+                nc.sync.dma_start(nodes[:], rows[:, 2 * u : 2 * u + 2, t0 : t0 + n])
+                raw[a, u, i] = nodes
                 t0 += n
             if (a, u) == (0, 0):
                 nc.sync.dma_start(offs_sb[:], offs)
         for a in range(PASSES):
-            nc.sync.dma_start(w_raw[a][:], w[512 * a : 512 * (a + 1), :].rearrange("(p j) m -> p j m", j=4))
+            nc.sync.dma_start(w_raw[a][:], w[K_PASS * a : K_PASS * (a + 1), :].rearrange("(p j) m -> p j m", j=4))
         nc.sync.dma_start(b_sb[:], b)
-        for tile, pos in zip(pos_sb, (pos1, pos2, pos3, pos4)):
-            nc.sync.dma_start(tile[:], pos)
-        for h in range(2):
-            nc.sync.dma_start(
-                gate_sb[:, :, V // 2 * h : V // 2 * (h + 1)],
-                gate.rearrange("d m v -> m d v")[:, :, V // 2 * h : V // 2 * (h + 1)],
-            )
+        for pos_tile, pos in zip(pos_sb, (pos1, pos2, pos3, pos4)):
+            nc.sync.dma_start(pos_tile[:], pos)
+        gate_rows = gate.rearrange("d m v -> m d v")
+        for half in range(2):
+            columns = slice(V // 2 * half, V // 2 * (half + 1))
+            nc.sync.dma_start(gate_sb[:, :, columns], gate_rows[:, :, columns])
 
         pair = {}
         for a in range(PASSES):
             for u in range(2):
                 pair[a, u] = keep.tile([P, T, 2], BF16, name=f"pair_{a}{u}", align_bytes=64)
-        G0, G1 = 512, 256
         picked = {}
-        for a, g in ((0, G0), (1, G1)):
-            for s in range(S // g):
-                picked[a, s] = keep.tile([P, g, 4], BF16, name=f"picked_{a}_{s}", align_bytes=64)
+        for a, n in ((0, SLICE0), (1, SLICE1)):
+            for s in range(S // n):
+                picked[a, s] = keep.tile([P, n, 4], BF16, name=f"picked_{a}_{s}", align_bytes=64)
         x_codes = [keep.tile([P, S], U32, name=f"x_codes{a}", align_bytes=64) for a in range(PASSES)]
         x_scales = [keep.tile([P, S], U8, name=f"x_scales{a}", align_bytes=64) for a in range(PASSES)]
         w_bf = [keep.tile([P, N, 4], BF16, name=f"w_bf{a}", align_bytes=64) for a in range(PASSES)]
         w_codes = [keep.tile([P, N], U32, name=f"w_codes{a}", align_bytes=64) for a in range(PASSES)]
         w_scales = [keep.tile([P, N], U8, name=f"w_scales{a}", align_bytes=64) for a in range(PASSES)]
 
-        def cast(a, u):
+        def round_nodes(a, u):
             t0 = 0
-            for i, (n, nv) in enumerate(LOADS[a, u]):
+            for i, (n, n_vector) in enumerate(LOADS[a, u]):
                 src = raw[a, u, i]
-                ns = n - nv
-                if ns:
+                n_scalar = n - n_vector
+                if n_scalar:
                     nc.scalar.activation(
-                        pair[a, u][:, t0 : t0 + ns, :], src[:, :, :ns].rearrange("p e t -> p t e"), COPY
+                        pair[a, u][:, t0 : t0 + n_scalar, :], src[:, :, :n_scalar].rearrange("p e t -> p t e"), COPY
                     )
-                if nv:
+                if n_vector:
                     nc.vector.tensor_copy(
-                        pair[a, u][:, t0 + ns : t0 + n, :], src[:, :, ns:].rearrange("p e t -> p t e")
+                        pair[a, u][:, t0 + n_scalar : t0 + n, :], src[:, :, n_scalar:].rearrange("p e t -> p t e")
                     )
                 t0 += n
 
-        def gather(a, u, s):
-            g = G0 if a == 0 else G1
+        def words_of(a, u, s):
+            columns = (SLICE0 if a == 0 else SLICE1) // LIST_ROWS
             words = pair[a, u][:].rearrange("p t e -> p (t e)").bitcast(U32)
-            dst = picked[a, s][:].rearrange("p s j -> p (s j)").bitcast(U32).rearrange("p (s u) -> p s u", u=2)
-            nc.vector.tensor_copy(dst[:, :, u], words.indirect(offs_sb[:, g // 16 * s : g // 16 * (s + 1)]))
+            return words.indirect(offs_sb[:, columns * s : columns * (s + 1)])
 
-        def quantize(a, tile, e0, e1, c0):
-            n = e1 - e0
+        def pick(a, u, s):
+            words = picked[a, s][:].rearrange("p s j -> p (s j)").bitcast(U32).rearrange("p (s u) -> p s u", u=2)
+            nc.vector.tensor_copy(words[:, :, u], words_of(a, u, s))
+
+        def pick_and_spread(s):
+            near = keep.tile([P, SLICE1, 2], BF16, name=f"near_{s}", align_bytes=64)
+            nc.vector.tensor_copy(near[:].rearrange("p s e -> p (s e)").bitcast(U32), words_of(1, 1, s))
+            nc.scalar.copy(picked[1, s][:, :, 2:4], near[:])
+
+        def quantize_nodes(a, nodes, j0, j1, column):
+            columns = slice(column, column + j1 - j0)
             nc.vector.quantize_mx(
-                out=x_codes[a][:, c0 : c0 + n].bitcast(FP8X4),
-                scales=x_scales[a][:, c0 : c0 + n],
-                in_=tile[:, e0:e1, :].rearrange("p s j -> p (s j)"),
+                out=x_codes[a][:, columns].bitcast(FP8X4),
+                scales=x_scales[a][:, columns],
+                in_=nodes[:, j0:j1, :].rearrange("p s j -> p (s j)"),
             )
-
-        cast(0, 0)
-        gather(0, 0, 0)
-        gather(0, 0, 1)
-        cast(0, 1)
-        gather(0, 1, 0)
-        gather(0, 1, 1)
-        cast(1, 0)
-        quantize(0, picked[0, 0], 0, 512, 0)
-        quantize(0, picked[0, 1], 0, 512, 512)
-        for s in range(4):
-            gather(1, 0, s)
-        cast(1, 1)
-        for a in range(PASSES):
-            nc.scalar.activation(w_bf[a][:], w_raw[a][:].rearrange("p j m -> p m j"), COPY)
 
         def quantize_w(a):
             nc.vector.quantize_mx(
                 out=w_codes[a][:].bitcast(FP8X4), scales=w_scales[a][:], in_=w_bf[a][:].rearrange("p m j -> p (m j)")
             )
 
-        def gather_and_spread(s):
-            near = keep.tile([P, G1, 2], BF16, name=f"near_{s}", align_bytes=64)
-            nc.vector.tensor_copy(
-                near[:].rearrange("p s e -> p (s e)").bitcast(U32),
-                pair[1, 1][:].rearrange("p t e -> p (t e)").bitcast(U32).indirect(offs_sb[:, G1 // 16 * s : G1 // 16 * (s + 1)]),
-            )
-            nc.scalar.copy(picked[1, s][:, :, 2:4], near[:])
+        for u in range(2):
+            round_nodes(0, u)
+            for s in range(S // SLICE0):
+                pick(0, u, s)
+        round_nodes(1, 0)
+        for s in range(S // SLICE0):
+            quantize_nodes(0, picked[0, s], 0, SLICE0, SLICE0 * s)
+        for s in range(S // SLICE1):
+            pick(1, 0, s)
 
-        gather_and_spread(0)
-        gather_and_spread(1)
-        quantize_w(0)
-        gather(1, 1, 2)
-        quantize_w(1)
-        gather(1, 1, 3)
-        quantize(1, picked[1, 0], 0, 256, 0)
-        quantize(1, picked[1, 1], 0, 256, 256)
-        quantize(1, picked[1, 2], 0, 256, 512)
-        quantize(1, picked[1, 3], 0, 128, 768)
-        quantize(1, picked[1, 3], 128, 256, 896)
+        round_nodes(1, 1)
+        for a in range(PASSES):
+            nc.scalar.activation(w_bf[a][:], w_raw[a][:].rearrange("p j m -> p m j"), COPY)
+        for s in range(SPREAD):
+            pick_and_spread(s)
+        for a in range(PASSES):
+            quantize_w(a)
+            pick(1, 1, SPREAD + a)
+        for column, n in BANKS:
+            s, j0 = divmod(column, SLICE1)
+            quantize_nodes(1, picked[1, s], j0, j0 + n, column)
 
         y = keep.tile([P, S], F32, name="y")
-        slices = [(0, 256), (256, 256), (512, 256), (768, 128), (896, 128)]
-        banks = [psum.tile([P, n], F32, name=f"bank{i}") for i, (c0, n) in enumerate(slices)]
+        banks = [psum.tile([P, n], F32, name=f"bank{i}") for i, (column, n) in enumerate(BANKS)]
         for a in range(PASSES):
-            for bank, (c0, n) in zip(banks, slices):
+            for bank, (column, n) in zip(banks, BANKS):
                 nc.tensor.matmul_mx(
                     out=bank[:],
                     lhsT=w_codes[a][:].bitcast(FP8X4),
                     lhsT_scale=w_scales[a][:],
-                    rhs=x_codes[a][:, c0 : c0 + n].bitcast(FP8X4),
-                    rhs_scale=x_scales[a][:, c0 : c0 + n],
+                    rhs=x_codes[a][:, column : column + n].bitcast(FP8X4),
+                    rhs_scale=x_scales[a][:, column : column + n],
                     start=(a == 0),
                     stop=(a == PASSES - 1),
                 )
-        for i, (bank, (c0, n)) in enumerate(zip(banks, slices)):
-            if i < 4:
-                nc.scalar.activation(y[:, c0 : c0 + n], bank[:], RELU, bias=b_sb[:])
+        for i, (bank, (column, n)) in enumerate(zip(banks, BANKS)):
+            if i < len(BANKS) - 1:
+                nc.scalar.activation(y[:, column : column + n], bank[:], RELU, bias=b_sb[:])
             else:
-                nc.vector.tensor_scalar(y[:, c0 : c0 + n], bank[:], b_sb[:], 0.0, ADD, MAX)
+                nc.vector.tensor_scalar(y[:, column : column + n], bank[:], b_sb[:], 0.0, ADD, MAX)
 
-        H = 384
-        prod = [keep.tile([P, V], F32, name=f"prod_{d}") for d in range(D)]
+        products = [keep.tile([P, V], F32, name=f"prod_{d}") for d in range(D)]
         sums = [keep.tile([P, V], F32, name=f"sum_{i}") for i in range(D - 1)]
 
-        def fetch(d, v0, v1):
-            nc.vector.tensor_tensor(
-                prod[d][:, v0:v1],
-                y[:].indirect(pos_sb[d][:, v0 // 16 : v1 // 16]),
-                gate_sb[:, d, v0:v1],
-                MULT,
-            )
+        def fetch(d):
+            nc.vector.tensor_tensor(products[d][:], y[:].indirect(pos_sb[d][:]), gate_sb[:, d, :], MULT)
 
         def add(i, v0, v1):
-            lhs = prod[0] if i == 0 else sums[i - 1]
-            nc.vector.tensor_tensor(sums[i][:, v0:v1], lhs[:, v0:v1], prod[i + 1][:, v0:v1], ADD)
+            so_far = products[0] if i == 0 else sums[i - 1]
+            nc.vector.tensor_tensor(sums[i][:, v0:v1], so_far[:, v0:v1], products[i + 1][:, v0:v1], ADD)
 
-        fetch(0, 0, V)
-        fetch(1, 0, V)
-        fetch(2, 0, V)
+        fetch(0)
+        fetch(1)
+        fetch(2)
         add(0, 0, V)
-        fetch(3, 0, V)
-        add(1, 0, H)
-        add(1, H, V)
-        add(2, 0, H)
-        nc.sync.dma_start(out[:, :H], sums[2][:, :H])
-        add(2, H, V)
-        nc.scalar.dma_start(out[:, H:], sums[2][:, H:])
+        fetch(3)
+        add(1, 0, SPLIT)
+        add(1, SPLIT, V)
+        add(2, 0, SPLIT)
+        nc.sync.dma_start(out[:, :SPLIT], sums[2][:, :SPLIT])
+        add(2, SPLIT, V)
+        nc.scalar.dma_start(out[:, SPLIT:], sums[2][:, SPLIT:])

from contextlib import ExitStack

import concourse.mybir as mybir

K, T, D, S, V, N = 1024, 2048, 4, 1024, 512, 128
FLOPS = 2 * K * S * N + 2 * D * V * N

F32 = mybir.dt.float32
BF16 = mybir.dt.bfloat16
U32 = mybir.dt.uint32
U16 = mybir.dt.uint16
U8 = mybir.dt.uint8
FP8X4 = mybir.dt.float8_e4m3fn_x4
COPY = mybir.ActivationFunctionType.Copy
RELU = mybir.ActivationFunctionType.Relu
ADD = mybir.AluOpType.add
MAX = mybir.AluOpType.max
MULT = mybir.AluOpType.mult

P = 128
PASSES = 2
K_PASS = K // PASSES
LIST_ROWS = 16

LOADS = {
    (0, 0): [(512, 320), (512, 320), (512, 320), (512, 320)],
    (0, 1): [(512, 128), (512, 160), (512, 128), (512, 288)],
    (1, 0): [(512, 0), (512, 0), (512, 0), (512, 192)],
    (1, 1): [(512, 0), (512, 0), (512, 256), (256, 0), (256, 128)],
}

SLICE0 = 512
SLICE1 = 256
SPREAD = 2

BANKS = [(0, 256), (256, 256), (512, 256), (768, 128), (896, 128)]

SPLIT = 384


def tile_picked_sub_lin_relu_sub_e_kernel(tc, xT, w, b, gate, offs, pos1, pos2, pos3, pos4, out):
    nc = tc.nc
    with ExitStack() as ctx:
        keep = ctx.enter_context(tc.tile_pool(name="keep", bufs=1))
        psum = ctx.enter_context(tc.psum_pool(name="psum", bufs=1))

        warm = keep.tile([P, 1], F32, name="warm")
        warm_out = keep.tile([P, 1], F32, name="warm_out")
        nc.vector.memset(warm[:], 0.0)
        nc.scalar.activation(warm_out[:], warm[:], RELU)

        offs_sb = keep.tile([P, S // LIST_ROWS], U16, name="offs_sb")
        pos_sb = [keep.tile([P, V // LIST_ROWS], U16, name=f"pos_sb{d}") for d in range(D)]
        b_sb = keep.tile([P, 1], F32, name="b_sb")
        w_raw = [keep.tile([P, 4, N], F32, name=f"w_raw{a}") for a in range(PASSES)]
        gate_sb = keep.tile([P, D, V], F32, name="gate_sb")

        raw = {}
        for (a, u), loads in LOADS.items():
            rows = xT[K_PASS * a : K_PASS * (a + 1), :].rearrange("(p j) t -> p j t", j=4)
            t0 = 0
            for i, (n, n_vector) in enumerate(loads):
                nodes = keep.tile([P, 2, n], F32, name=f"raw_{a}{u}_{i}")
                nc.sync.dma_start(nodes[:], rows[:, 2 * u : 2 * u + 2, t0 : t0 + n])
                raw[a, u, i] = nodes
                t0 += n
            if (a, u) == (0, 0):
                nc.sync.dma_start(offs_sb[:], offs)
        for a in range(PASSES):
            nc.sync.dma_start(w_raw[a][:], w[K_PASS * a : K_PASS * (a + 1), :].rearrange("(p j) m -> p j m", j=4))
        nc.sync.dma_start(b_sb[:], b)
        for pos_tile, pos in zip(pos_sb, (pos1, pos2, pos3, pos4)):
            nc.sync.dma_start(pos_tile[:], pos)
        gate_rows = gate.rearrange("d m v -> m d v")
        for half in range(2):
            columns = slice(V // 2 * half, V // 2 * (half + 1))
            nc.sync.dma_start(gate_sb[:, :, columns], gate_rows[:, :, columns])

        pair = {}
        for a in range(PASSES):
            for u in range(2):
                pair[a, u] = keep.tile([P, T, 2], BF16, name=f"pair_{a}{u}", align_bytes=64)
        picked = {}
        for a, n in ((0, SLICE0), (1, SLICE1)):
            for s in range(S // n):
                picked[a, s] = keep.tile([P, n, 4], BF16, name=f"picked_{a}_{s}", align_bytes=64)
        x_codes = [keep.tile([P, S], U32, name=f"x_codes{a}", align_bytes=64) for a in range(PASSES)]
        x_scales = [keep.tile([P, S], U8, name=f"x_scales{a}", align_bytes=64) for a in range(PASSES)]
        w_bf = [keep.tile([P, N, 4], BF16, name=f"w_bf{a}", align_bytes=64) for a in range(PASSES)]
        w_codes = [keep.tile([P, N], U32, name=f"w_codes{a}", align_bytes=64) for a in range(PASSES)]
        w_scales = [keep.tile([P, N], U8, name=f"w_scales{a}", align_bytes=64) for a in range(PASSES)]

        def round_nodes(a, u):
            t0 = 0
            for i, (n, n_vector) in enumerate(LOADS[a, u]):
                src = raw[a, u, i]
                n_scalar = n - n_vector
                if n_scalar:
                    nc.scalar.activation(
                        pair[a, u][:, t0 : t0 + n_scalar, :], src[:, :, :n_scalar].rearrange("p e t -> p t e"), COPY
                    )
                if n_vector:
                    nc.vector.tensor_copy(
                        pair[a, u][:, t0 + n_scalar : t0 + n, :], src[:, :, n_scalar:].rearrange("p e t -> p t e")
                    )
                t0 += n

        def words_of(a, u, s):
            columns = (SLICE0 if a == 0 else SLICE1) // LIST_ROWS
            words = pair[a, u][:].rearrange("p t e -> p (t e)").bitcast(U32)
            return words.indirect(offs_sb[:, columns * s : columns * (s + 1)])

        def pick(a, u, s):
            words = picked[a, s][:].rearrange("p s j -> p (s j)").bitcast(U32).rearrange("p (s u) -> p s u", u=2)
            nc.vector.tensor_copy(words[:, :, u], words_of(a, u, s))

        def pick_and_spread(s):
            near = keep.tile([P, SLICE1, 2], BF16, name=f"near_{s}", align_bytes=64)
            nc.vector.tensor_copy(near[:].rearrange("p s e -> p (s e)").bitcast(U32), words_of(1, 1, s))
            nc.scalar.copy(picked[1, s][:, :, 2:4], near[:])

        def quantize_nodes(a, nodes, j0, j1, column):
            columns = slice(column, column + j1 - j0)
            nc.vector.quantize_mx(
                out=x_codes[a][:, columns].bitcast(FP8X4),
                scales=x_scales[a][:, columns],
                in_=nodes[:, j0:j1, :].rearrange("p s j -> p (s j)"),
            )

        def quantize_w(a):
            nc.vector.quantize_mx(
                out=w_codes[a][:].bitcast(FP8X4), scales=w_scales[a][:], in_=w_bf[a][:].rearrange("p m j -> p (m j)")
            )

        for u in range(2):
            round_nodes(0, u)
            for s in range(S // SLICE0):
                pick(0, u, s)
        round_nodes(1, 0)
        for s in range(S // SLICE0):
            quantize_nodes(0, picked[0, s], 0, SLICE0, SLICE0 * s)
        for s in range(S // SLICE1):
            pick(1, 0, s)

        round_nodes(1, 1)
        for a in range(PASSES):
            nc.scalar.activation(w_bf[a][:], w_raw[a][:].rearrange("p j m -> p m j"), COPY)
        for s in range(SPREAD):
            pick_and_spread(s)
        for a in range(PASSES):
            quantize_w(a)
            pick(1, 1, SPREAD + a)
        for column, n in BANKS:
            s, j0 = divmod(column, SLICE1)
            quantize_nodes(1, picked[1, s], j0, j0 + n, column)

        y = keep.tile([P, S], F32, name="y")
        banks = [psum.tile([P, n], F32, name=f"bank{i}") for i, (column, n) in enumerate(BANKS)]
        for a in range(PASSES):
            for bank, (column, n) in zip(banks, BANKS):
                nc.tensor.matmul_mx(
                    out=bank[:],
                    lhsT=w_codes[a][:].bitcast(FP8X4),
                    lhsT_scale=w_scales[a][:],
                    rhs=x_codes[a][:, column : column + n].bitcast(FP8X4),
                    rhs_scale=x_scales[a][:, column : column + n],
                    start=(a == 0),
                    stop=(a == PASSES - 1),
                )
        for i, (bank, (column, n)) in enumerate(zip(banks, BANKS)):
            if i < len(BANKS) - 1:
                nc.scalar.activation(y[:, column : column + n], bank[:], RELU, bias=b_sb[:])
            else:
                nc.vector.tensor_scalar(y[:, column : column + n], bank[:], b_sb[:], 0.0, ADD, MAX)

        products = [keep.tile([P, V], F32, name=f"prod_{d}") for d in range(D)]
        sums = [keep.tile([P, V], F32, name=f"sum_{i}") for i in range(D - 1)]

        def fetch(d):
            nc.vector.tensor_tensor(products[d][:], y[:].indirect(pos_sb[d][:]), gate_sb[:, d, :], MULT)

        def add(i, v0, v1):
            so_far = products[0] if i == 0 else sums[i - 1]
            nc.vector.tensor_tensor(sums[i][:, v0:v1], so_far[:, v0:v1], products[i + 1][:, v0:v1], ADD)

        fetch(0)
        fetch(1)
        fetch(2)
        add(0, 0, V)
        fetch(3)
        add(1, 0, SPLIT)
        add(1, SPLIT, V)
        add(2, 0, SPLIT)
        nc.sync.dma_start(out[:, :SPLIT], sums[2][:, :SPLIT])
        add(2, SPLIT, V)
        nc.scalar.dma_start(out[:, SPLIT:], sums[2][:, SPLIT:])
